import numpy as np
import ml_dtypes


def mxq(x, axis, fmt="e4m3"):
    dtype, down = {"e4m3": (ml_dtypes.float8_e4m3fn, 7), "e5m2": (ml_dtypes.float8_e5m2, 14)}[fmt]
    v = np.moveaxis(np.asarray(x, np.float32).astype(ml_dtypes.bfloat16).astype(np.float64), axis, -1)
    blocks = v.reshape(v.shape[:-1] + (-1, 32))
    amax = np.abs(blocks).max(-1, keepdims=True)
    byte = np.maximum(np.where(amax > 0, np.frexp(amax)[1] - 1 + 127, 0) - down, 1)
    scale = np.exp2(byte - 127.0)
    codes = (blocks / scale).astype(np.float32).astype(dtype).astype(np.float64)
    return np.moveaxis((codes * scale).reshape(v.shape), -1, axis)


WIDE = False


def mx_kscale(k):
    if not WIDE:
        return np.ones(k)
    levels = np.array([10, -10, 5, -5, 0])
    if k % 512:
        return np.exp2(np.random.permutation(np.resize(levels, k // 32))).repeat(32)
    a = np.empty((k // 512, 16))
    for p in range(k // 512):
        a[p, :8] = np.random.permutation(np.resize(levels, 8))
        for g in range(8):
            far = levels[np.abs(levels - a[p, g]) >= 10]
            a[p, g + 8] = far[np.random.randint(len(far))]
    return np.exp2(a.ravel()).repeat(32)


def f64(x):
    return np.asarray(x).astype(np.float64)


def striped(idx):
    return np.tile(idx.reshape(-1, 16).T, (8, 1)).astype(np.uint16)


def unstriped(offs):
    return offs[:16].T.reshape(-1).astype(np.int64)


E2M1 = np.array([0.0, 0.5, 1.0, 1.5, 2.0, 3.0, 4.0, 6.0, -0.0, -0.5, -1.0, -1.5, -2.0, -3.0, -4.0, -6.0])


def pack_weight(w, fmt):
    k, n = w.shape
    w = f64(np.asarray(w, np.float32).astype(ml_dtypes.bfloat16)).reshape(k // 32, 32, n)
    amax = np.abs(w).max(1)
    if fmt == "e4m3":
        byte = np.frexp(amax)[1] - 1 + 127 - 7
    else:
        mant, ex = np.frexp(amax / 6.0)
        byte = np.where(mant > 0.5, ex, ex - 1) + 127
    byte = np.clip(np.where(amax > 0, byte, 1), 1, 254)
    scaled = (w * np.exp2(127.0 - byte)[:, None, :]).reshape(k, n).astype(np.float32)
    by_word = np.ascontiguousarray(scaled.reshape(k // 512, 128, 4, n).transpose(0, 1, 3, 2))
    if fmt == "e4m3":
        words = by_word.astype(ml_dtypes.float8_e4m3fn).view(np.uint8)
    else:
        c = by_word.astype(ml_dtypes.float4_e2m1fn).view(np.uint8) & 0xF
        words = (c[..., 0::2] | (c[..., 1::2] << 4)).reshape(k // 512, 128, 2 * n)
    return np.ascontiguousarray(words), np.ascontiguousarray(byte.astype(np.uint8).reshape(k // 512, 16, n))


def unpack_weight(words, scales, fmt):
    g, _, n = scales.shape
    words = np.ascontiguousarray(words).reshape(g, 128, n, -1)
    if fmt == "e4m3":
        vals = words.view(ml_dtypes.float8_e4m3fn).astype(np.float64)
    else:
        nib = np.empty((g, 128, n, 4), np.uint8)
        nib[..., 0::2] = words & 0xF
        nib[..., 1::2] = words >> 4
        vals = E2M1[nib]
    vals = vals * np.repeat(np.exp2(scales.astype(np.float64) - 127.0), 8, axis=1)[..., None]
    return vals.transpose(0, 1, 3, 2).reshape(g * 512, n)


def pack_table(v):
    words, scales = pack_weight(v, "e4m3")
    return np.concatenate([words.reshape(words.shape[0], -1), scales.reshape(scales.shape[0], -1)], axis=1)


def unpack_table(tab):
    g, t = tab.shape[0], tab.shape[1] // 528
    return unpack_weight(tab[:, :512 * t].reshape(g, 128, t, 4), tab[:, 512 * t:].reshape(g, 16, t), "e4m3")


K, M, T, S = 512, 512, 2048, 1024


def setup_inputs():
    n = np.random.standard_normal
    s = mx_kscale(K)[:, None]
    return {
        "tab": pack_table(n((K, T)) * s),
        "w": (n((K, M)) / np.sqrt(K) / s).astype(np.float32),
        "wgo": np.tile(np.random.uniform(0.5, 2.0, S), (128, 1)).astype(np.float32),
        "offs": striped(np.random.permutation(T)[:S]),
        "offs2": striped(np.random.permutation(T)[:S]),
    }


def reference(tab, w, wgo, offs, offs2):
    tab_ = unpack_table(tab)[:, unstriped(offs)]
    w_ = mxq(f64(w), 0, "e4m3")
    y = w_.T @ tab_
    out = np.zeros((M, T))
    out[:, unstriped(offs2)] = f64(wgo)[0] * (y)
    return out

@@ -1,0 +1,114 @@
+from contextlib import ExitStack
+
+import concourse.mybir as mybir
+
+K, M, T, S = 512, 512, 2048, 1024
+FLOPS = 2 * K * M * S
+
+F32 = mybir.dt.float32
+BF16 = mybir.dt.bfloat16
+I32 = mybir.dt.int32
+U32 = mybir.dt.uint32
+U16 = mybir.dt.uint16
+U8 = mybir.dt.uint8
+FP8X4 = mybir.dt.float8_e4m3fn_x4
+MULT = mybir.AluOpType.mult
+
+P = 128
+PACK = 4
+HALF = 512
+
+
+def tile_list_tabscat_none_kernel(tc, tab, w, wgo, offs, offs2, out):
+    nc = tc.nc
+    with ExitStack() as ctx:
+        held = ctx.enter_context(tc.tile_pool(name="held", bufs=1))
+        psum = ctx.enter_context(tc.psum_pool(name="psum", bufs=1))
+
+        offsets = held.tile([P, S // 16], U16, name="offsets")
+        offsets2 = held.tile([P, S // 16], U16, name="offsets2")
+        scales = held.tile([P, T // 4], I32, name="scales", align_bytes=64)
+        words = held.tile([P, T], I32, name="words", align_bytes=64)
+        picked_words = held.tile([P, S], U32, name="picked_words", align_bytes=64)
+        picked_scales = held.tile([P, S], U8, name="picked_scales", align_bytes=64)
+        weights = held.tile([P, S], F32, name="weights")
+        windows = [held.tile([P, T], F32, name=f"window{b}") for b in range(2)]
+
+        nc.vector.memset(scales[:], 0)
+        for b in range(2):
+            (nc.vector if b < 1 else nc.gpsimd).memset(windows[b][:], 0.0)
+
+        tab_words = tab[0, 0 : K * T].rearrange("(p b) -> p b", p=P).bitcast(I32)
+        tab_scales = tab[0, K * T : K * T + 16 * T].rearrange("(q t) -> q t", q=16).bitcast(I32)
+        nc.sync.dma_start(offsets[:], offs)
+        for q in range(4):
+            nc.sync.dma_start(out=scales[32 * q : 32 * q + 4, :], in_=tab_scales[4 * q : 4 * q + 4, :])
+        nc.sync.dma_start(out=words[:], in_=tab_words)
+
+        w_rows = w.rearrange("(p j) c -> p j c", j=PACK)
+        bounds = ((0, 128), (128, 512))
+        raws = []
+        for c0, c1 in bounds:
+            raw = held.tile([P, PACK, c1 - c0], F32, name=f"raw{c0}")
+            raws.append(raw)
+        nc.sync.dma_start(out=raws[0][:], in_=w_rows[:, :, 0:128])
+        nc.sync.dma_start(offsets2[:], offs2)
+        nc.sync.dma_start(out=weights[:], in_=wgo)
+        nc.sync.dma_start(out=raws[1][:], in_=w_rows[:, :, 128:512])
+
+        codes = [held.tile([P, P], U32, name=f"codes{m}", align_bytes=64) for m in range(4)]
+        planes = [held.tile([P, P], U8, name=f"planes{m}", align_bytes=64) for m in range(4)]
+
+        def group(m):
+            grouped = held.tile([P, P, PACK], BF16, name=f"grouped{m}", align_bytes=64)
+            src = raws[0][:] if m == 0 else raws[1][:, :, (m - 1) * P : m * P]
+            nc.scalar.copy(out=grouped[:], in_=src.rearrange("p j c -> p c j"))
+            return grouped
+
+        def quant(m, grouped):
+            nc.vector.quantize_mx(
+                out=codes[m][:].bitcast(FP8X4),
+                scales=planes[m][:],
+                in_=grouped[:].rearrange("p c j -> p (c j)"),
+            )
+
+        def pick(dst, src, a, b):
+            nc.vector.tensor_copy(out=dst[:, a:b], in_=src.indirect(offsets[:, a // 16 : b // 16]))
+
+        def product(m, h):
+            cols = slice(h * HALF, (h + 1) * HALF)
+            acc = psum.tile([P, HALF], F32, name=f"acc{m}{h}")
+            nc.tensor.matmul_mx(
+                out=acc[:],
+                lhsT=codes[m][:].bitcast(FP8X4),
+                lhsT_scale=planes[m][:],
+                rhs=picked_words[:, cols].bitcast(FP8X4),
+                rhs_scale=picked_scales[:, cols],
+                start=True,
+                stop=True,
+            )
+            return acc
+
+        pick(picked_scales, scales[:].bitcast(U8), 0, S)
+        g0 = group(0)
+        pick(picked_words, words[:].bitcast(U32), 0, HALF)
+        quant(0, g0)
+        pick(picked_words, words[:].bitcast(U32), HALF, S)
+
+        for m in range(4):
+            if m > 0:
+                quant(m, group(m))
+            y = held.tile([P, S], F32, name=f"y{m}")
+            window = windows[m % 2]
+            for h in range(2):
+                acc = product(m, h)
+                cols = slice(h * HALF, (h + 1) * HALF)
+                nc.scalar.copy(out=y[:, cols], in_=acc[:])
+            if m == 0:
+                for h in range(2):
+                    cols = slice(h * HALF, (h + 1) * HALF)
+                    ocols = slice(h * HALF // 16, (h + 1) * HALF // 16)
+                    nc.vector.tensor_tensor(window[:].indirect(offsets2[:, ocols]), y[:, cols], weights[:, cols], MULT)
+            else:
+                nc.vector.tensor_tensor(window[:].indirect(offsets2[:]), y[:, 0:S], weights[:, 0:S], MULT)
+            nc.sync.dma_start(out=out[m * P : (m + 1) * P, :], in_=window[:])

@@ -16,7 +16,6 @@ MULT = mybir.AluOpType.mult
 
 P = 128
 PACK = 4
-HALF = 512
 
 
 def tile_list_tabscat_none_kernel(tc, tab, w, wgo, offs, offs2, out):
@@ -34,81 +33,80 @@ def tile_list_tabscat_none_kernel(tc, tab, w, wgo, offs, offs2, out):
         weights = held.tile([P, S], F32, name="weights")
         windows = [held.tile([P, T], F32, name=f"window{b}") for b in range(2)]
 
-        nc.vector.memset(scales[:], 0)
-        for b in range(2):
-            (nc.vector if b < 1 else nc.gpsimd).memset(windows[b][:], 0.0)
+        nc.gpsimd.memset(scales[:], 0)
+        nc.vector.memset(windows[0][:], 0.0)
+        nc.gpsimd.memset(windows[1][:], 0.0)
 
         tab_words = tab[0, 0 : K * T].rearrange("(p b) -> p b", p=P).bitcast(I32)
         tab_scales = tab[0, K * T : K * T + 16 * T].rearrange("(q t) -> q t", q=16).bitcast(I32)
+        w_rows = w.rearrange("(p j) c -> p j c", j=PACK)
+        w_chunks = ((0, 128), (128, 512))
+        raws = [held.tile([P, PACK, c1 - c0], F32, name=f"raw{c0}") for c0, c1 in w_chunks]
+
+        def load_w(i):
+            nc.sync.dma_start(out=raws[i][:], in_=w_rows[:, :, w_chunks[i][0] : w_chunks[i][1]])
+
         nc.sync.dma_start(offsets[:], offs)
+
         for q in range(4):
             nc.sync.dma_start(out=scales[32 * q : 32 * q + 4, :], in_=tab_scales[4 * q : 4 * q + 4, :])
+        load_w(0)
         nc.sync.dma_start(out=words[:], in_=tab_words)
-
-        w_rows = w.rearrange("(p j) c -> p j c", j=PACK)
-        bounds = ((0, 128), (128, 512))
-        raws = []
-        for c0, c1 in bounds:
-            raw = held.tile([P, PACK, c1 - c0], F32, name=f"raw{c0}")
-            raws.append(raw)
-        nc.sync.dma_start(out=raws[0][:], in_=w_rows[:, :, 0:128])
         nc.sync.dma_start(offsets2[:], offs2)
         nc.sync.dma_start(out=weights[:], in_=wgo)
-        nc.sync.dma_start(out=raws[1][:], in_=w_rows[:, :, 128:512])
+        load_w(1)
 
-        codes = [held.tile([P, P], U32, name=f"codes{m}", align_bytes=64) for m in range(4)]
-        planes = [held.tile([P, P], U8, name=f"planes{m}", align_bytes=64) for m in range(4)]
+        codes = held.tile([P, M], U32, name="codes", align_bytes=64)
+        planes = held.tile([P, M], U8, name="planes", align_bytes=64)
+        grouped = held.tile([P, M, PACK], BF16, name="grouped", align_bytes=64)
 
-        def group(m):
-            grouped = held.tile([P, P, PACK], BF16, name=f"grouped{m}", align_bytes=64)
-            src = raws[0][:] if m == 0 else raws[1][:, :, (m - 1) * P : m * P]
-            nc.scalar.copy(out=grouped[:], in_=src.rearrange("p j c -> p c j"))
-            return grouped
-
-        def quant(m, grouped):
+        def prepare_w(i, a, b):
+            c0 = w_chunks[i][0]
+            nc.scalar.copy(out=grouped[:, a:b, :], in_=raws[i][:, :, a - c0 : b - c0].rearrange("p j c -> p c j"))
             nc.vector.quantize_mx(
-                out=codes[m][:].bitcast(FP8X4),
-                scales=planes[m][:],
-                in_=grouped[:].rearrange("p c j -> p (c j)"),
+                out=codes[:, a:b].bitcast(FP8X4),
+                scales=planes[:, a:b],
+                in_=grouped[:, a:b, :].rearrange("p c j -> p (c j)"),
             )
 
         def pick(dst, src, a, b):
             nc.vector.tensor_copy(out=dst[:, a:b], in_=src.indirect(offsets[:, a // 16 : b // 16]))
 
-        def product(m, h):
-            cols = slice(h * HALF, (h + 1) * HALF)
-            acc = psum.tile([P, HALF], F32, name=f"acc{m}{h}")
+        banks = [0]
+
+        def product(m, y, a, b):
+            acc = psum.tile([P, b - a], F32, name=f"acc{banks[0] % 8}")
+            banks[0] += 1
             nc.tensor.matmul_mx(
                 out=acc[:],
-                lhsT=codes[m][:].bitcast(FP8X4),
-                lhsT_scale=planes[m][:],
-                rhs=picked_words[:, cols].bitcast(FP8X4),
-                rhs_scale=picked_scales[:, cols],
+                lhsT=codes[:, m * P : (m + 1) * P].bitcast(FP8X4),
+                lhsT_scale=planes[:, m * P : (m + 1) * P],
+                rhs=picked_words[:, a:b].bitcast(FP8X4),
+                rhs_scale=picked_scales[:, a:b],
                 start=True,
                 stop=True,
             )
-            return acc
+            nc.scalar.copy(out=y[:, a:b], in_=acc[:])
 
+        def place(m, y, a, b):
+            nc.vector.tensor_tensor(
+                windows[m % 2][:].indirect(offsets2[:, a // 16 : b // 16]), y[:, a:b], weights[:, a:b], MULT
+            )
+
+        pieces = ((0, 256), (256, 1024))
         pick(picked_scales, scales[:].bitcast(U8), 0, S)
-        g0 = group(0)
-        pick(picked_words, words[:].bitcast(U32), 0, HALF)
-        quant(0, g0)
-        pick(picked_words, words[:].bitcast(U32), HALF, S)
-
+        prepare_w(0, 0, 128)
+        ys = [held.tile([P, S], F32, name=f"y{m}") for m in range(4)]
+        for a, b in pieces:
+            pick(picked_words, words[:].bitcast(U32), a, b)
+            for c in range(a, b, 512):
+                product(0, ys[0], c, min(c + 512, b))
         for m in range(4):
             if m > 0:
-                quant(m, group(m))
-            y = held.tile([P, S], F32, name=f"y{m}")
-            window = windows[m % 2]
-            for h in range(2):
-                acc = product(m, h)
-                cols = slice(h * HALF, (h + 1) * HALF)
-                nc.scalar.copy(out=y[:, cols], in_=acc[:])
-            if m == 0:
-                for h in range(2):
-                    cols = slice(h * HALF, (h + 1) * HALF)
-                    ocols = slice(h * HALF // 16, (h + 1) * HALF // 16)
-                    nc.vector.tensor_tensor(window[:].indirect(offsets2[:, ocols]), y[:, cols], weights[:, cols], MULT)
-            else:
-                nc.vector.tensor_tensor(window[:].indirect(offsets2[:]), y[:, 0:S], weights[:, 0:S], MULT)
-            nc.sync.dma_start(out=out[m * P : (m + 1) * P, :], in_=window[:])
+                if m < 3:
+                    prepare_w(1, *((128, 256) if m == 1 else (256, 512)))
+                for a, b in ((0, 512), (512, 1024)):
+                    product(m, ys[m], a, b)
+            for a, b in pieces if m == 0 else ((0, S),):
+                place(m, ys[m], a, b)
+            nc.sync.dma_start(out=out[m * P : (m + 1) * P, :], in_=windows[m % 2][:])

@@ -40,7 +40,7 @@ def tile_list_tabscat_none_kernel(tc, tab, w, wgo, offs, offs2, out):
         tab_words = tab[0, 0 : K * T].rearrange("(p b) -> p b", p=P).bitcast(I32)
         tab_scales = tab[0, K * T : K * T + 16 * T].rearrange("(q t) -> q t", q=16).bitcast(I32)
         w_rows = w.rearrange("(p j) c -> p j c", j=PACK)
-        w_chunks = ((0, 128), (128, 512))
+        w_chunks = ((0, 256), (256, 512))
         raws = [held.tile([P, PACK, c1 - c0], F32, name=f"raw{c0}") for c0, c1 in w_chunks]
 
         def load_w(i):
@@ -51,10 +51,10 @@ def tile_list_tabscat_none_kernel(tc, tab, w, wgo, offs, offs2, out):
         for q in range(4):
             nc.sync.dma_start(out=scales[32 * q : 32 * q + 4, :], in_=tab_scales[4 * q : 4 * q + 4, :])
         load_w(0)
+        load_w(1)
         nc.sync.dma_start(out=words[:], in_=tab_words)
         nc.sync.dma_start(offsets2[:], offs2)
         nc.sync.dma_start(out=weights[:], in_=wgo)
-        load_w(1)
 
         codes = held.tile([P, M], U32, name="codes", align_bytes=64)
         planes = held.tile([P, M], U8, name="planes", align_bytes=64)
@@ -95,7 +95,8 @@ def tile_list_tabscat_none_kernel(tc, tab, w, wgo, offs, offs2, out):
 
         pieces = ((0, 256), (256, 1024))
         pick(picked_scales, scales[:].bitcast(U8), 0, S)
-        prepare_w(0, 0, 128)
+        prepare_w(0, 0, 256)
+        prepare_w(1, 256, 512)
         ys = [held.tile([P, S], F32, name=f"y{m}") for m in range(4)]
         for a, b in pieces:
             pick(picked_words, words[:].bitcast(U32), a, b)
@@ -103,8 +104,6 @@ def tile_list_tabscat_none_kernel(tc, tab, w, wgo, offs, offs2, out):
                 product(0, ys[0], c, min(c + 512, b))
         for m in range(4):
             if m > 0:
-                if m < 3:
-                    prepare_w(1, *((128, 256) if m == 1 else (256, 512)))
                 for a, b in ((0, 512), (512, 1024)):
                     product(m, ys[m], a, b)
             for a, b in pieces if m == 0 else ((0, S),):

from contextlib import ExitStack

import concourse.mybir as mybir

K, M, T, S = 512, 512, 2048, 1024
FLOPS = 2 * K * M * S

F32 = mybir.dt.float32
BF16 = mybir.dt.bfloat16
I32 = mybir.dt.int32
U32 = mybir.dt.uint32
U16 = mybir.dt.uint16
U8 = mybir.dt.uint8
FP8X4 = mybir.dt.float8_e4m3fn_x4
MULT = mybir.AluOpType.mult

P = 128
PACK = 4


def tile_list_tabscat_none_kernel(tc, tab, w, wgo, offs, offs2, out):
    nc = tc.nc
    with ExitStack() as ctx:
        held = ctx.enter_context(tc.tile_pool(name="held", bufs=1))
        psum = ctx.enter_context(tc.psum_pool(name="psum", bufs=1))

        offsets = held.tile([P, S // 16], U16, name="offsets")
        offsets2 = held.tile([P, S // 16], U16, name="offsets2")
        scales = held.tile([P, T // 4], I32, name="scales", align_bytes=64)
        words = held.tile([P, T], I32, name="words", align_bytes=64)
        picked_words = held.tile([P, S], U32, name="picked_words", align_bytes=64)
        picked_scales = held.tile([P, S], U8, name="picked_scales", align_bytes=64)
        weights = held.tile([P, S], F32, name="weights")
        windows = [held.tile([P, T], F32, name=f"window{b}") for b in range(2)]

        nc.gpsimd.memset(scales[:], 0)
        nc.vector.memset(windows[0][:], 0.0)
        nc.gpsimd.memset(windows[1][:], 0.0)

        tab_words = tab[0, 0 : K * T].rearrange("(p b) -> p b", p=P).bitcast(I32)
        tab_scales = tab[0, K * T : K * T + 16 * T].rearrange("(q t) -> q t", q=16).bitcast(I32)
        w_rows = w.rearrange("(p j) c -> p j c", j=PACK)
        w_chunks = ((0, 256), (256, 512))
        raws = [held.tile([P, PACK, c1 - c0], F32, name=f"raw{c0}") for c0, c1 in w_chunks]

        def load_w(i):
            nc.sync.dma_start(out=raws[i][:], in_=w_rows[:, :, w_chunks[i][0] : w_chunks[i][1]])

        nc.sync.dma_start(offsets[:], offs)

        for q in range(4):
            nc.sync.dma_start(out=scales[32 * q : 32 * q + 4, :], in_=tab_scales[4 * q : 4 * q + 4, :])
        load_w(0)
        load_w(1)
        nc.sync.dma_start(out=words[:], in_=tab_words)
        nc.sync.dma_start(offsets2[:], offs2)
        nc.sync.dma_start(out=weights[:], in_=wgo)

        codes = held.tile([P, M], U32, name="codes", align_bytes=64)
        planes = held.tile([P, M], U8, name="planes", align_bytes=64)
        grouped = held.tile([P, M, PACK], BF16, name="grouped", align_bytes=64)

        def prepare_w(i, a, b):
            c0 = w_chunks[i][0]
            nc.scalar.copy(out=grouped[:, a:b, :], in_=raws[i][:, :, a - c0 : b - c0].rearrange("p j c -> p c j"))
            nc.vector.quantize_mx(
                out=codes[:, a:b].bitcast(FP8X4),
                scales=planes[:, a:b],
                in_=grouped[:, a:b, :].rearrange("p c j -> p (c j)"),
            )

        def pick(dst, src, a, b):
            nc.vector.tensor_copy(out=dst[:, a:b], in_=src.indirect(offsets[:, a // 16 : b // 16]))

        banks = [0]

        def product(m, y, a, b):
            acc = psum.tile([P, b - a], F32, name=f"acc{banks[0] % 8}")
            banks[0] += 1
            nc.tensor.matmul_mx(
                out=acc[:],
                lhsT=codes[:, m * P : (m + 1) * P].bitcast(FP8X4),
                lhsT_scale=planes[:, m * P : (m + 1) * P],
                rhs=picked_words[:, a:b].bitcast(FP8X4),
                rhs_scale=picked_scales[:, a:b],
                start=True,
                stop=True,
            )
            nc.scalar.copy(out=y[:, a:b], in_=acc[:])

        def place(m, y, a, b):
            nc.vector.tensor_tensor(
                windows[m % 2][:].indirect(offsets2[:, a // 16 : b // 16]), y[:, a:b], weights[:, a:b], MULT
            )

        pieces = ((0, 256), (256, 1024))
        pick(picked_scales, scales[:].bitcast(U8), 0, S)
        prepare_w(0, 0, 256)
        prepare_w(1, 256, 512)
        ys = [held.tile([P, S], F32, name=f"y{m}") for m in range(4)]
        for a, b in pieces:
            pick(picked_words, words[:].bitcast(U32), a, b)
            for c in range(a, b, 512):
                product(0, ys[0], c, min(c + 512, b))
        for m in range(4):
            if m > 0:
                for a, b in ((0, 512), (512, 1024)):
                    product(m, ys[m], a, b)
            for a, b in pieces if m == 0 else ((0, S),):
                place(m, ys[m], a, b)
            nc.sync.dma_start(out=out[m * P : (m + 1) * P, :], in_=windows[m % 2][:])
